import numpy as np
import ml_dtypes


def mxq(x, axis, fmt="e4m3"):
    dtype, down = {"e4m3": (ml_dtypes.float8_e4m3fn, 7), "e5m2": (ml_dtypes.float8_e5m2, 14)}[fmt]
    v = np.moveaxis(np.asarray(x, np.float32).astype(ml_dtypes.bfloat16).astype(np.float64), axis, -1)
    blocks = v.reshape(v.shape[:-1] + (-1, 32))
    amax = np.abs(blocks).max(-1, keepdims=True)
    byte = np.maximum(np.where(amax > 0, np.frexp(amax)[1] - 1 + 127, 0) - down, 1)
    scale = np.exp2(byte - 127.0)
    codes = (blocks / scale).astype(np.float32).astype(dtype).astype(np.float64)
    return np.moveaxis((codes * scale).reshape(v.shape), -1, axis)


WIDE = False


def mx_kscale(k):
    if not WIDE:
        return np.ones(k)
    levels = np.array([10, -10, 5, -5, 0])
    if k % 512:
        return np.exp2(np.random.permutation(np.resize(levels, k // 32))).repeat(32)
    a = np.empty((k // 512, 16))
    for p in range(k // 512):
        a[p, :8] = np.random.permutation(np.resize(levels, 8))
        for g in range(8):
            far = levels[np.abs(levels - a[p, g]) >= 10]
            a[p, g + 8] = far[np.random.randint(len(far))]
    return np.exp2(a.ravel()).repeat(32)


BF16 = ml_dtypes.bfloat16


def bf(x):
    return np.asarray(x, np.float32).astype(BF16)


def f64(x):
    return np.asarray(x).astype(np.float64)


E2M1 = np.array([0.0, 0.5, 1.0, 1.5, 2.0, 3.0, 4.0, 6.0, -0.0, -0.5, -1.0, -1.5, -2.0, -3.0, -4.0, -6.0])


def pack_weight(w, fmt):
    k, n = w.shape
    w = f64(bf(w)).reshape(k // 32, 32, n)
    amax = np.abs(w).max(1)
    if fmt == "e4m3":
        byte = np.frexp(amax)[1] - 1 + 127 - 7
    else:
        mant, ex = np.frexp(amax / 6.0)
        byte = np.where(mant > 0.5, ex, ex - 1) + 127
    byte = np.clip(np.where(amax > 0, byte, 1), 1, 254)
    scaled = (w * np.exp2(127.0 - byte)[:, None, :]).reshape(k, n).astype(np.float32)
    by_word = np.ascontiguousarray(scaled.reshape(k // 512, 128, 4, n).transpose(0, 1, 3, 2))
    if fmt == "e4m3":
        words = by_word.astype(ml_dtypes.float8_e4m3fn).view(np.uint8)
    else:
        c = by_word.astype(ml_dtypes.float4_e2m1fn).view(np.uint8) & 0xF
        words = c[..., 0::2] | (c[..., 1::2] << 4)
    return np.ascontiguousarray(words), np.ascontiguousarray(byte.astype(np.uint8).reshape(k // 512, 16, n))


def unpack_weight(words, scales, fmt):
    g, p, n, _ = words.shape
    if fmt == "e4m3":
        vals = np.ascontiguousarray(words).view(ml_dtypes.float8_e4m3fn).astype(np.float64)
    else:
        nib = np.empty((g, p, n, 4), np.uint8)
        nib[..., 0::2] = words & 0xF
        nib[..., 1::2] = words >> 4
        vals = E2M1[nib]
    vals = vals * np.repeat(np.exp2(scales.astype(np.float64) - 127.0), 8, axis=1)[..., None]
    return vals.transpose(0, 1, 3, 2).reshape(g * 512, n)
def pack4(w):
    words, scales = pack_weight(w, "e2m1")
    return words.reshape(words.shape[0], 128, -1), scales


def unpack4(words, scales):
    return unpack_weight(words.reshape(words.shape[0], 128, -1, 2), scales, "e2m1")


E4M3FN = np.array([(-1.0 if i & 128 else 1.0) * ((1.0 + (i & 7) / 8.0) * 2.0 ** (((i >> 3) & 15) - 7) if i & 120 else (i & 7) * 2.0 ** -9) for i in range(256)])


def e4m3fn_bytes(y):
    return np.clip(np.asarray(y, np.float64), -448.0, 448.0).astype(np.float32).astype(ml_dtypes.float8_e4m3fn).view(np.uint8)


def e4m3fn_values(b):
    return E4M3FN[b]


N, K, D, F, P = 256, 4, 1024, 1024, 1024


def tanh_derivatives(th):
    d1 = 1.0 - th * th
    d2 = -2.0 * th * d1
    return d1, d2


def draw0():
    s, t = mx_kscale(D), mx_kscale(F)
    x = bf(np.random.standard_normal((N, D)) * s)
    j = bf(np.random.standard_normal((K, N, D)) / np.sqrt(K) * s)
    l = bf(np.random.standard_normal((N, D)) * s)
    w1_words, w1_scales = pack4(np.random.standard_normal((D, F)) / np.sqrt(D) / s[:, None])
    b = bf(0.5 * np.random.standard_normal(F))
    g = bf((1.0 + 0.1 * np.random.standard_normal(F)) * t)
    w2_words, w2_scales = pack4(np.random.standard_normal((F, P)) / np.sqrt(F) / t[:, None])
    return {"x": x,
            "j": j,
            "l": l,
            "w1_words": w1_words,
            "w1_scales": w1_scales,
            "b": b,
            "g": g,
            "w2_words": w2_words,
            "w2_scales": w2_scales}


def core(x, j, l, w1_words, w1_scales, b, g, w2_words, w2_scales):
    gain = f64(g)
    w1q = unpack4(w1_words, w1_scales)
    w2q = unpack4(w2_words, w2_scales)

    a = (mxq(f64(x), 1, "e4m3") @ w1q) + f64(b)
    th = np.tanh(a)

    ja = mxq(f64(j), 2, "e4m3") @ w1q

    la = mxq(f64(l), 1, "e4m3") @ w1q

    d1, d2 = tanh_derivatives(th)

    lh = d1 * la + d2 * np.sum(ja * ja, axis=0)

    lap = mxq(lh * gain, 1, "e4m3") @ w2q

    y = mxq(th * gain, 1, "e4m3") @ w2q
    return lap, y


def setup_inputs():
    drawn = draw0()
    full = np.asarray(drawn['j']).astype(np.float64)
    scale = (np.abs(full).reshape(4, 256, 8, 128).max(axis=(3,)) / 448.0).astype(np.float32)
    given = {}
    for key, value in drawn.items():
        if key == 'j':
            given['j_bytes'] = e4m3fn_bytes(full / np.repeat(scale.astype(np.float64), 128, axis=2))
            given['j_scale'] = scale
        else:
            given[key] = value
    return given


def reference(x, j_bytes, j_scale, l, w1_words, w1_scales, b, g, w2_words, w2_scales):
    return core(x, e4m3fn_values(j_bytes) * np.repeat(j_scale.astype(np.float64), 128, axis=2), l, w1_words, w1_scales, b, g, w2_words, w2_scales)

@@ -1,0 +1,467 @@
+from contextlib import ExitStack
+
+import concourse.mybir as mybir
+from concourse.masks import make_identity
+
+F32 = mybir.dt.float32
+BF16 = mybir.dt.bfloat16
+U8 = mybir.dt.uint8
+I32 = mybir.dt.int32
+U32 = mybir.dt.uint32
+FP8 = mybir.dt.float8_e4m3fn
+FP8X4 = mybir.dt.float8_e4m3fn_x4
+FP4X4 = mybir.dt.float4_e2m1fn_x4
+ALU = mybir.AluOpType
+ACT = mybir.ActivationFunctionType
+
+P = 128
+TOKENS, COORDS, D, F, OUT = 256, 4, 1024, 1024, 1024
+FLOPS = 2 * (COORDS + 2) * TOKENS * D * F + 2 * 2 * TOKENS * F * OUT
+
+
+def tile_forwardlaplaciantanhlayer_d1p_kernel(
+    tc, x, j_bytes, j_scale, l, w1_words, w1_scales, b, g, w2_words, w2_scales, out_lap, out_y
+):
+    nc = tc.nc
+    with ExitStack() as ctx:
+        sb = ctx.enter_context(tc.tile_pool(name="sb", bufs=1))
+        ps = ctx.enter_context(tc.psum_pool(name="ps", bufs=1))
+
+        def tile(name, shape, dtype):
+            return sb.tile(shape, dtype, name=name, align_bytes=64)
+
+        banks = [ps.tile([P, 512], F32, name="bank%d" % i) for i in range(8)]
+
+        ident = tile("ident", [P, P], F32)
+        warm = tile("warm", [P, 2], F32)
+        jsc = tile("jsc", [P, COORDS, 2, 8], F32)
+        jraw = [[tile("jraw%d%d" % (h, cp), [P, 2, D], U8) for cp in range(2)] for h in range(2)]
+        jrow = [[tile("jrow%d%d" % (h, c), [P, D], BF16) for c in range(COORDS)] for h in range(2)]
+        xall = tile("xall", [P, 2, D], BF16)
+        xrow = [xall[:, h] for h in range(2)]
+        lall = tile("lall", [P, 2, D], BF16)
+        lrow = [lall[:, h] for h in range(2)]
+        xgrp = tile("xgrp", [P, 2, 2, P, 4], BF16)
+        lgrp = tile("lgrp", [P, 2, 2, P, 4], BF16)
+        jgrp = [tile("jgrp%d" % h, [P, 2, COORDS, P, 4], BF16) for h in range(2)]
+        xc, xs = tile("xc", [P, 2, 2, P], U32), tile("xs", [P, 2, 2, P], U8)
+        lc, ls = tile("lc", [P, 2, 2, P], U32), tile("ls", [P, 2, 2, P], U8)
+        jc = [tile("jc%d" % h, [P, 2, COORDS * P], U32) for h in range(2)]
+        js = [tile("js%d" % h, [P, 2, COORDS * P], U8) for h in range(2)]
+        w1raw = [tile("w1raw%d" % G, [P, 2, 1024], U8) for G in range(2)]
+        w1sraw = tile("w1sraw", [P, 2, F], U8)
+        w1c = [tile("w1c%d" % G, [P, 2, 4, 2 * P], U8) for G in range(2)]
+        w1s = [tile("w1s%d" % G, [P, 2, 4, P], U8) for G in range(2)]
+        w2c = tile("w2c", [P, 2, 2 * OUT], U8)
+        w2s = tile("w2s", [P, 2, OUT], U8)
+        bcol = tile("bcol", [P, 2, 4], BF16)
+        gcol = tile("gcol", [P, 2, 4], BF16)
+        gpos = tile("gpos", [P, 2, 4], F32)
+        gneg = tile("gneg", [P, 2, 4], F32)
+        th = [tile("th%d" % G, [P, 4, TOKENS], F32) for G in range(2)]
+        th2 = [tile("th2%d" % G, [P, 4, TOKENS], F32) for G in range(2)]
+        d1g = [tile("d1g%d" % G, [P, 4, TOKENS], F32) for G in range(2)]
+        thg = tile("thg", [P, 2, TOKENS, 4], BF16)
+        tc_, ts_ = tile("thc", [P, 2, TOKENS], U32), tile("ths", [P, 2, TOKENS], U8)
+        sqr = [[tile("sqr%d%d" % (h, G), [P, 4, COORDS, P], F32) for G in range(2)] for h in range(2)]
+        half = [[tile("half%d%d" % (h, G), [P, 4, 2, P], F32) for G in range(2)] for h in range(2)]
+        ssum = [[tile("ssum%d%d" % (h, G), [P, 4, P], F32) for G in range(2)] for h in range(2)]
+        prod = [[tile("prod%d%d" % (h, G), [P, 4, P], F32) for G in range(2)] for h in range(2)]
+        inner = [[tile("inner%d%d" % (h, G), [P, 4, P], F32) for G in range(2)] for h in range(2)]
+        lhg = [tile("lhg%d" % h, [P, 2, P, 4], BF16) for h in range(2)]
+        hc = [tile("hc%d" % h, [P, 2, P], U32) for h in range(2)]
+        hs = [tile("hs%d" % h, [P, 2, P], U8) for h in range(2)]
+        res = [tile("res%d" % i, [P, 512], F32) for i in range(8)]
+
+        def rows(h):
+            return slice(h * P, (h + 1) * P)
+
+        def load_scales(eng, plane, scales):
+            for q in range(4):
+                eng.dma_start(
+                    out=plane[32 * q : 32 * q + 4, :, :].bitcast(I32),
+                    in_=scales[:, 4 * q : 4 * q + 4, :].rearrange("g r n -> r g n").bitcast(I32),
+                )
+
+        def load_j(h, cp):
+            nc.sync.dma_start(out=jraw[h][cp][:], in_=j_bytes[2 * cp : 2 * cp + 2, rows(h), :].rearrange("c p k -> p c k"))
+
+        def load_w1(G):
+            nc.sync.dma_start(
+                out=w1raw[G][:].bitcast(I32),
+                in_=w1_words[:, :, 1024 * G : 1024 * (G + 1)].rearrange("g p n -> p g n").bitcast(I32),
+            )
+
+        def permute_words(G):
+            nc.vector.tensor_copy(
+                out=w1c[G][:].rearrange("p g t (m e) -> p g t m e", e=2),
+                in_=w1raw[G][:].rearrange("p g (m t e) -> p g t m e", t=4, e=2),
+            )
+
+        def permute_scales(G):
+            nc.vector.tensor_copy(
+                out=w1s[G][:], in_=w1sraw[:, :, 512 * G : 512 * (G + 1)].rearrange("p g (m t) -> p g t m", t=4)
+            )
+
+        def widen(h, c, gp, on_vector):
+            for i in range(4 * gp, 4 * gp + 4):
+                cols = slice(i * P, (i + 1) * P)
+                src = jraw[h][c // 2][:, c % 2, cols].bitcast(FP8)
+                scale = jsc[:, c, h, i : i + 1]
+                if on_vector:
+                    nc.vector.tensor_scalar(out=jrow[h][c][:, cols], in0=src, scalar1=scale, scalar2=None, op0=ALU.mult)
+                else:
+                    nc.scalar.activation(out=jrow[h][c][:, cols], in_=src, func=ACT.Copy, scale=scale)
+
+        def turn(row, bank):
+            words = row[:].bitcast(F32)
+            for gp in range(2):
+                for u in range(2):
+                    s = 2 * gp + u
+                    nc.tensor.transpose(bank[:, s * P : (s + 1) * P], words[:, 256 * gp + u : 256 * (gp + 1) : 2], ident[:])
+
+        def empty(dst, bank, on_vector):
+            out = dst.bitcast(F32)
+            src = bank[:].rearrange("p (g u r) -> p g r u", g=2, u=2)
+            if on_vector:
+                nc.vector.tensor_copy(out=out, in_=src)
+            else:
+                nc.scalar.copy(out=out, in_=src)
+
+        def quant(codes, scales, src):
+            nc.vector.quantize_mx(out=codes.bitcast(FP8X4), scales=scales, in_=src)
+
+        def stage1(out, G, t, codes, scales):
+            for gp in range(2):
+                nc.tensor.matmul_mx(
+                    out=out,
+                    lhsT=w1c[G][:, gp, t, :].bitcast(FP4X4),
+                    lhsT_scale=w1s[G][:, gp, t, :],
+                    rhs=codes[:, gp, :].bitcast(FP8X4),
+                    rhs_scale=scales[:, gp, :],
+                    start=(gp == 0),
+                    stop=(gp == 1),
+                )
+
+        def mm_a(G, tp, bank):
+            for t in (2 * tp, 2 * tp + 1):
+                for h in range(2):
+                    s = 2 * (t % 2) + h
+                    stage1(bank[:, s * P : (s + 1) * P], G, t, xc[:, h], xs[:, h])
+
+        def tanh(G, tp, bank):
+            for t in (2 * tp, 2 * tp + 1):
+                nc.scalar.activation(
+                    out=th[G][:, t, :], in_=bank[:, (t % 2) * 256 : (t % 2 + 1) * 256], func=ACT.Tanh, bias=bcol[:, G, t : t + 1]
+                )
+
+        def square_th(G, tp):
+            ts = slice(2 * tp, 2 * tp + 2)
+            nc.scalar.activation(out=th2[G][:, ts], in_=th[G][:, ts], func=ACT.Square)
+
+        def slope(G, tp, on_vector):
+            for t in (2 * tp, 2 * tp + 1):
+                neg, pos = gneg[:, G, t : t + 1], gpos[:, G, t : t + 1]
+                if on_vector:
+                    nc.vector.tensor_scalar(
+                        out=d1g[G][:, t, :], in0=th2[G][:, t, :], scalar1=neg, scalar2=pos, op0=ALU.mult, op1=ALU.add
+                    )
+                else:
+                    nc.scalar.activation(out=d1g[G][:, t, :], in_=th2[G][:, t, :], func=ACT.Identity, scale=neg, bias=pos)
+
+        def gains():
+            nc.vector.tensor_copy(out=gpos[:], in_=gcol[:])
+            nc.vector.tensor_scalar(out=gneg[:], in0=gcol[:], scalar1=-1.0, scalar2=None, op0=ALU.mult)
+
+        def gain_th(G, h):
+            nc.vector.tensor_tensor(
+                out=thg[:, G, rows(h)].rearrange("p (c i) t -> p c t i", i=4),
+                in0=th[G][:, :, rows(h)].rearrange("p t (c i) -> p c t i", i=4),
+                in1=gpos[:, G, :].unsqueeze(1).unsqueeze(3).to_broadcast([P, P // 4, 4, 4]),
+                op=ALU.mult,
+            )
+
+        def quant_th(G):
+            quant(tc_[:, G, :], ts_[:, G, :], thg[:, G].rearrange("p r t -> p (r t)"))
+
+        def quant_x(h):
+            quant(xc[:, h].rearrange("p g r -> p (g r)"), xs[:, h].rearrange("p g r -> p (g r)"), flat(xgrp[:, h]))
+
+        def mm_l(h, G, bank):
+            for t in range(4):
+                stage1(bank[:, t * P : (t + 1) * P], G, t, lc[:, h], ls[:, h])
+
+        def mm_j(h, G, t, bank):
+            stage1(bank[:], G, t, jc[h], js[h])
+
+        def square_j(h, G, t, bank):
+            nc.scalar.activation(out=sqr[h][G][:, t].rearrange("p c r -> p (c r)"), in_=bank[:], func=ACT.Square)
+
+        def mm_jt(h, G, c, bank):
+            for gp in range(2):
+                nc.tensor.matmul_mx(
+                    out=bank[:],
+                    lhsT=jc[h][:, gp, c * P : (c + 1) * P].bitcast(FP8X4),
+                    lhsT_scale=js[h][:, gp, c * P : (c + 1) * P],
+                    rhs=w1raw[G][:, gp, :].bitcast(FP4X4),
+                    rhs_scale=w1sraw[:, gp, 512 * G : 512 * (G + 1)],
+                    start=(gp == 0),
+                    stop=(gp == 1),
+                )
+
+        def square_jt(h, G, c, bank):
+            nc.scalar.activation(out=sqr[h][G][:, c], in_=bank[:].rearrange("p (m t) -> p t m", t=4), func=ACT.Square)
+
+        def sum_turn(h, G, bank, ts):
+            for t in range(ts.start, ts.stop):
+                for c in range(COORDS):
+                    nc.tensor.matmul(
+                        bank[:, t * P : (t + 1) * P], lhsT=sqr[h][G][:, c, t, :], rhs=ident[:], start=(c == 0), stop=(c == COORDS - 1),
+                        is_transpose=True,
+                    )
+
+        def curve_ps(h, G, bank, ts):
+            nc.vector.scalar_tensor_tensor(
+                out=prod[h][G][:, ts], in0=bank[:].rearrange("p (t r) -> p t r", t=4)[:, ts], scalar=-2.0, in1=th[G][:, ts, rows(h)],
+                op0=ALU.mult, op1=ALU.mult,
+            )
+
+        def add_pairs(h, G, tp):
+            ts = slice(2 * tp, 2 * tp + 2)
+            nc.vector.tensor_tensor(out=half[h][G][:, ts], in0=sqr[h][G][:, ts, 0:2], in1=sqr[h][G][:, ts, 2:4], op=ALU.add)
+
+        def add_halves(h, G, ts):
+            nc.vector.tensor_tensor(out=ssum[h][G][:, ts], in0=half[h][G][:, ts, 0], in1=half[h][G][:, ts, 1], op=ALU.add)
+
+        def curve(h, G, ts):
+            nc.vector.scalar_tensor_tensor(
+                out=prod[h][G][:, ts], in0=ssum[h][G][:, ts], scalar=-2.0, in1=th[G][:, ts, rows(h)], op0=ALU.mult, op1=ALU.mult
+            )
+
+        def add_la(h, G, bank, ts):
+            nc.vector.tensor_tensor(
+                out=inner[h][G][:, ts], in0=bank[:].rearrange("p (t r) -> p t r", t=4)[:, ts], in1=prod[h][G][:, ts], op=ALU.add
+            )
+
+        def gain_lh(h, G):
+            nc.vector.tensor_tensor(
+                out=lhg[h][:, G].rearrange("p (c i) t -> p c t i", i=4),
+                in0=inner[h][G][:].rearrange("p t (c i) -> p c t i", i=4),
+                in1=d1g[G][:, :, rows(h)].rearrange("p t (c i) -> p c t i", i=4),
+                op=ALU.mult,
+            )
+
+        def stage2(bank, codes, scales, nh, G):
+            nc.tensor.matmul_mx(
+                out=bank[:],
+                lhsT=codes.bitcast(FP8X4),
+                lhsT_scale=scales,
+                rhs=w2c[:, G, 1024 * nh : 1024 * (nh + 1)].bitcast(FP4X4),
+                rhs_scale=w2s[:, G, 512 * nh : 512 * (nh + 1)],
+                start=(G == 0),
+                stop=(G == 1),
+            )
+
+        def mm_y(h, nh, bank):
+            for G in range(2):
+                stage2(bank, tc_[:, G, rows(h)], ts_[:, G, rows(h)], nh, G)
+
+        def mm_lap(h, nh, G, bank):
+            stage2(bank, hc[h][:, G, :], hs[h][:, G, :], nh, G)
+
+        def store(dst, h, nh, bank, slot, on_vector):
+            if on_vector:
+                nc.vector.tensor_copy(out=res[slot][:], in_=bank[:])
+            else:
+                nc.scalar.copy(out=res[slot][:], in_=bank[:])
+            nc.sync.dma_start(out=dst[rows(h), 512 * nh : 512 * (nh + 1)], in_=res[slot][:])
+
+        def flat(ap):
+            return ap.rearrange("p a r t -> p (a r t)")
+
+        def quant_j(h, gp):
+            quant(jc[h][:, gp, :], js[h][:, gp, :], flat(jgrp[h][:, gp]))
+
+        def quant_l(h):
+            quant(lc[:, h].rearrange("p g r -> p (g r)"), ls[:, h].rearrange("p g r -> p (g r)"), flat(lgrp[:, h]))
+
+        def quant_lh(h, G):
+            quant(hc[h][:, G, :], hs[h][:, G, :], lhg[h][:, G].rearrange("p r t -> p (r t)"))
+
+        B = banks
+        V, S = True, False
+        with tc.manual_schedule():
+            nc.vector.memset(w1sraw[:].bitcast(U32), 0)
+            nc.vector.memset(warm[:, 0:1], 0.0)
+            nc.vector.memset(w2s[:].bitcast(U32), 0)
+            nc.sync.dma_start(out=jsc[:], in_=j_scale.rearrange("c (h p) i -> p c h i", p=P))
+            load_j(0, 0)
+            load_w1(0)
+            nc.sync.dma_start(out=xall[:], in_=x.rearrange("(h p) k -> p h k", p=P))
+            load_scales(nc.scalar, w1sraw, w1_scales)
+            nc.scalar.activation(out=warm[:, 1:2], in_=warm[:, 0:1], func=ACT.Tanh)
+            make_identity(nc, ident[:])
+            nc.gpsimd.dma_start(out=bcol[:], in_=b.rearrange("(G p t) -> p G t", p=P, t=4))
+            nc.gpsimd.dma_start(out=gcol[:], in_=g.rearrange("(G p t) -> p G t", p=P, t=4))
+            load_j(0, 1)
+            load_w1(1)
+            load_j(1, 0)
+            load_j(1, 1)
+            nc.sync.dma_start(out=lall[:], in_=l.rearrange("(h p) k -> p h k", p=P))
+            nc.sync.dma_start(out=w2c[:].bitcast(I32), in_=w2_words.rearrange("g p n -> p g n").bitcast(I32))
+            load_scales(nc.sync, w2s, w2_scales)
+            widen(0, 0, 0, S)
+            widen(0, 0, 1, V)
+            widen(0, 1, 0, S)
+            widen(0, 1, 1, S)
+            turn(jrow[0][0], B[0])
+            permute_words(0)
+            permute_scales(0)
+            widen(0, 2, 0, V)
+            widen(0, 3, 1, V)
+            widen(0, 3, 0, S)
+            turn(xrow[0], B[1])
+            empty(xgrp[:, 0], B[1], S)
+            widen(0, 2, 1, V)
+            turn(jrow[0][1], B[2])
+            widen(1, 0, 0, V)
+            turn(xrow[1], B[3])
+            widen(1, 2, 1, V)
+            turn(jrow[0][3], B[4])
+            widen(1, 2, 0, V)
+            widen(1, 0, 1, S)
+            empty(jgrp[0][:, :, 3], B[4], S)
+            gains()
+            turn(jrow[0][2], B[5])
+            turn(jrow[1][0], B[6])
+            turn(jrow[1][2], B[7])
+            empty(xgrp[:, 1], B[3], S)
+            turn(lrow[0], B[1])
+            widen(1, 3, 1, V)
+            widen(1, 1, 1, V)
+            widen(1, 3, 0, V)
+            empty(jgrp[1][:, :, 0], B[6], S)
+            turn(lrow[1], B[4])
+            quant_x(1)
+            turn(jrow[1][3], B[3])
+            widen(1, 1, 0, V)
+            empty(jgrp[0][:, :, 2], B[5], S)
+            empty(jgrp[1][:, :, 2], B[7], S)
+            quant_x(0)
+            turn(jrow[1][1], B[6])
+            empty(jgrp[0][:, :, 0], B[0], S)
+            mm_a(0, 0, B[5])
+            empty(jgrp[0][:, :, 1], B[2], S)
+            permute_scales(1)
+            permute_words(1)
+            empty(jgrp[1][:, :, 3], B[3], S)
+            mm_a(0, 1, B[7])
+            quant_j(0, 1)
+            quant_j(0, 0)
+            tanh(0, 0, B[5])
+            mm_a(1, 1, B[0])
+            mm_a(1, 0, B[2])
+            empty(jgrp[1][:, :, 1], B[6], S)
+            quant_j(1, 1)
+            mm_j(0, 0, 0, B[3])
+            tanh(0, 1, B[7])
+            square_th(0, 0)
+            quant_j(1, 0)
+            mm_jt(0, 1, 2, B[5])
+            tanh(1, 1, B[0])
+            square_j(0, 0, 0, B[3])
+            gain_th(0, 1)
+            empty(lgrp[:, 1], B[4], V)
+            tanh(1, 0, B[2])
+            slope(0, 0, V)
+            mm_j(1, 0, 2, B[6])
+            mm_j(0, 0, 3, B[7])
+            mm_j(0, 0, 1, B[0])
+            empty(lgrp[:, 0], B[1], S)
+            mm_j(0, 0, 2, B[3])
+            square_j(0, 0, 1, B[0])
+            gain_th(0, 0)
+            gain_th(1, 0)
+            quant_th(0)
+            square_th(0, 1)
+            mm_jt(0, 1, 0, B[4])
+            quant_l(0)
+            slope(0, 1, V)
+            mm_j(1, 0, 3, B[2])
+            gain_th(1, 1)
+            quant_l(1)
+            square_j(0, 0, 3, B[7])
+            mm_jt(1, 1, 3, B[1])
+            mm_jt(1, 1, 0, B[0])
+            square_j(1, 0, 2, B[6])
+            add_pairs(0, 0, 0)
+            mm_j(1, 0, 0, B[7])
+            square_j(0, 0, 2, B[3])
+            square_j(1, 0, 3, B[2])
+            quant_th(1)
+            square_j(1, 0, 0, B[7])
+            mm_j(1, 0, 1, B[6])
+            add_pairs(1, 0, 1)
+            mm_l(0, 0, B[3])
+            mm_jt(1, 1, 2, B[2])
+            square_j(1, 0, 1, B[6])
+            add_pairs(0, 0, 1)
+            square_jt(0, 1, 2, B[5])
+            add_pairs(1, 0, 0)
+            square_jt(0, 1, 0, B[4])
+            mm_jt(0, 1, 1, B[7])
+            square_th(1, 0)
+            add_halves(0, 0, slice(0, 4))
+            mm_jt(1, 1, 1, B[6])
+            mm_jt(0, 1, 3, B[5])
+            square_jt(0, 1, 1, B[7])
+            add_halves(1, 0, slice(0, 4))
+            curve(0, 0, slice(0, 4))
+            curve(1, 0, slice(0, 4))
+            mm_y(1, 0, B[4])
+            square_jt(0, 1, 3, B[5])
+            mm_l(1, 0, B[7])
+            square_jt(1, 1, 3, B[1])
+            mm_l(0, 1, B[5])
+            add_la(0, 0, B[3], slice(0, 4))
+            square_jt(1, 1, 0, B[0])
+            add_la(1, 0, B[7], slice(0, 4))
+            sum_turn(0, 1, B[1], slice(0, 4))
+            square_jt(1, 1, 2, B[2])
+            square_jt(1, 1, 1, B[6])
+            sum_turn(1, 1, B[3], slice(0, 4))
+            slope(1, 0, S)
+            mm_y(1, 1, B[0])
+            square_th(1, 1)
+            mm_l(1, 1, B[7])
+            store(out_y, 1, 0, B[4], 2, S)
+            gain_lh(0, 0)
+            mm_y(0, 0, B[2])
+            gain_lh(1, 0)
+            slope(1, 1, S)
+            mm_y(0, 1, B[6])
+            quant_lh(0, 0)
+            curve_ps(0, 1, B[1], slice(0, 4))
+            quant_lh(1, 0)
+            add_la(0, 1, B[5], slice(0, 4))
+            curve_ps(1, 1, B[3], slice(0, 4))
+            gain_lh(0, 1)
+            mm_lap(0, 0, 0, B[1])
+            add_la(1, 1, B[7], slice(0, 4))
+            store(out_y, 1, 1, B[0], 3, S)
+            quant_lh(0, 1)
+            store(out_y, 0, 0, B[2], 0, S)
+            mm_lap(0, 1, 0, B[4])
+            mm_lap(0, 0, 1, B[1])
+            mm_lap(1, 0, 0, B[5])
+            mm_lap(0, 1, 1, B[4])
+            gain_lh(1, 1)
+            store(out_y, 0, 1, B[6], 1, S)
+            store(out_lap, 0, 0, B[1], 4, S)
+            quant_lh(1, 1)
+            mm_lap(1, 0, 1, B[5])
+            mm_lap(1, 1, 0, B[3])
+            store(out_lap, 0, 1, B[4], 5, V)
+            store(out_lap, 1, 0, B[5], 6, S)
+            mm_lap(1, 1, 1, B[3])
+            store(out_lap, 1, 1, B[3], 7, S)

@@ -61,6 +61,8 @@ def tile_forwardlaplaciantanhlayer_d1p_kernel(
         th = [tile("th%d" % G, [P, 4, TOKENS], F32) for G in range(2)]
         th2 = [tile("th2%d" % G, [P, 4, TOKENS], F32) for G in range(2)]
         d1g = [tile("d1g%d" % G, [P, 4, TOKENS], F32) for G in range(2)]
+        thp = tile("thp", [P, 2, 4, TOKENS], BF16)
+        zeros = tile("zeros", [P, 512], BF16)
         thg = tile("thg", [P, 2, TOKENS, 4], BF16)
         tc_, ts_ = tile("thc", [P, 2, TOKENS], U32), tile("ths", [P, 2, TOKENS], U8)
         sqr = [[tile("sqr%d%d" % (h, G), [P, 4, COORDS, P], F32) for G in range(2)] for h in range(2)]
@@ -84,7 +86,7 @@ def tile_forwardlaplaciantanhlayer_d1p_kernel(
                 )
 
         def load_j(h, cp):
-            nc.sync.dma_start(out=jraw[h][cp][:], in_=j_bytes[2 * cp : 2 * cp + 2, rows(h), :].rearrange("c p k -> p c k"))
+            nc.sync.dma_start(out=jraw[h][cp][:], in_=j_bytes[2 * cp : 2 * cp + 2].rearrange("c (p h) k -> p c h k", h=2)[:, :, h, :])
 
         def load_w1(G):
             nc.sync.dma_start(
@@ -103,13 +105,28 @@ def tile_forwardlaplaciantanhlayer_d1p_kernel(
                 out=w1s[G][:], in_=w1sraw[:, :, 512 * G : 512 * (G + 1)].rearrange("p g (m t) -> p g t m", t=4)
             )
 
+        split = set()
+
+        def turn_j(h, c, bank):
+            words = jrow[h][c][:].bitcast(F32)
+            for gp in range(2):
+                for u in range(2):
+                    s = 2 * gp + u
+                    src = words[:, s * P : (s + 1) * P] if (h, c, gp) in split else words[:, 256 * gp + u : 256 * (gp + 1) : 2]
+                    nc.tensor.transpose(bank[:, s * P : (s + 1) * P], src, ident[:])
+
         def widen(h, c, gp, on_vector):
             for i in range(4 * gp, 4 * gp + 4):
                 cols = slice(i * P, (i + 1) * P)
                 src = jraw[h][c // 2][:, c % 2, cols].bitcast(FP8)
                 scale = jsc[:, c, h, i : i + 1]
                 if on_vector:
-                    nc.vector.tensor_scalar(out=jrow[h][c][:, cols], in0=src, scalar1=scale, scalar2=None, op0=ALU.mult)
+                    split.add((h, c, gp))
+                    dst = jrow[h][c][:, 512 * gp : 512 * (gp + 1)].rearrange("p (u m e) -> p m u e", u=2, e=2)
+                    nc.vector.tensor_scalar(
+                        out=dst[:, 32 * (i % 4) : 32 * (i % 4 + 1)], in0=src.rearrange("p (m u e) -> p m u e", u=2, e=2),
+                        scalar1=scale, scalar2=None, op0=ALU.mult,
+                    )
                 else:
                     nc.scalar.activation(out=jrow[h][c][:, cols], in_=src, func=ACT.Copy, scale=scale)
 
@@ -173,13 +190,21 @@ def tile_forwardlaplaciantanhlayer_d1p_kernel(
             nc.vector.tensor_copy(out=gpos[:], in_=gcol[:])
             nc.vector.tensor_scalar(out=gneg[:], in0=gcol[:], scalar1=-1.0, scalar2=None, op0=ALU.mult)
 
-        def gain_th(G, h):
-            nc.vector.tensor_tensor(
-                out=thg[:, G, rows(h)].rearrange("p (c i) t -> p c t i", i=4),
-                in0=th[G][:, :, rows(h)].rearrange("p t (c i) -> p c t i", i=4),
-                in1=gpos[:, G, :].unsqueeze(1).unsqueeze(3).to_broadcast([P, P // 4, 4, 4]),
-                op=ALU.mult,
+        def gain_th(G, tp, on_vector):
+            for t in (2 * tp, 2 * tp + 1):
+                pos = gpos[:, G, t : t + 1]
+                if on_vector:
+                    nc.vector.tensor_scalar(out=thp[:, G, t, :], in0=th[G][:, t, :], scalar1=pos, scalar2=None, op0=ALU.mult)
+                else:
+                    nc.scalar.activation(out=thp[:, G, t, :], in_=th[G][:, t, :], func=ACT.Copy, scale=pos)
+
+        def weave_th(G):
+            nc.vector.tensor_copy(
+                out=thg[:, G].rearrange("p (c i) t -> p c t i", i=4), in_=thp[:, G].rearrange("p t (c i) -> p c t i", i=4)
             )
+
+        def warm_pe(bank):
+            nc.tensor.matmul(bank[:], lhsT=zeros[:, 0:P], rhs=zeros[:], start=True, stop=True)
 
         def quant_th(G):
             quant(tc_[:, G, :], ts_[:, G, :], thg[:, G].rearrange("p r t -> p (r t)"))
@@ -274,7 +299,7 @@ def tile_forwardlaplaciantanhlayer_d1p_kernel(
                 nc.vector.tensor_copy(out=res[slot][:], in_=bank[:])
             else:
                 nc.scalar.copy(out=res[slot][:], in_=bank[:])
-            nc.sync.dma_start(out=dst[rows(h), 512 * nh : 512 * (nh + 1)], in_=res[slot][:])
+            nc.sync.dma_start(out=dst.rearrange("(p h) n -> p h n", h=2)[:, h, 512 * nh : 512 * (nh + 1)], in_=res[slot][:])
 
         def flat(ap):
             return ap.rearrange("p a r t -> p (a r t)")
@@ -291,177 +316,190 @@ def tile_forwardlaplaciantanhlayer_d1p_kernel(
         B = banks
         V, S = True, False
         with tc.manual_schedule():
+            nc.vector.memset(zeros[:], 0.0)
             nc.vector.memset(w1sraw[:].bitcast(U32), 0)
-            nc.vector.memset(warm[:, 0:1], 0.0)
+            nc.vector.memset(ident[:], 0.0)
             nc.vector.memset(w2s[:].bitcast(U32), 0)
-            nc.sync.dma_start(out=jsc[:], in_=j_scale.rearrange("c (h p) i -> p c h i", p=P))
+            nc.sync.dma_start(out=jsc[:], in_=j_scale.rearrange("c (p h) i -> p c h i", h=2))
             load_j(0, 0)
             load_w1(0)
-            nc.sync.dma_start(out=xall[:], in_=x.rearrange("(h p) k -> p h k", p=P))
+            nc.sync.dma_start(out=xall[:], in_=x.rearrange("(p h) k -> p h k", h=2))
             load_scales(nc.scalar, w1sraw, w1_scales)
-            nc.scalar.activation(out=warm[:, 1:2], in_=warm[:, 0:1], func=ACT.Tanh)
-            make_identity(nc, ident[:])
-            nc.gpsimd.dma_start(out=bcol[:], in_=b.rearrange("(G p t) -> p G t", p=P, t=4))
-            nc.gpsimd.dma_start(out=gcol[:], in_=g.rearrange("(G p t) -> p G t", p=P, t=4))
+            nc.scalar.activation(out=warm[:, 0:1], in_=zeros[:, 0:1], func=ACT.Tanh)
+            make_identity(nc, ident[:], nomemset=True)
             load_j(0, 1)
             load_w1(1)
             load_j(1, 0)
             load_j(1, 1)
-            nc.sync.dma_start(out=lall[:], in_=l.rearrange("(h p) k -> p h k", p=P))
+            nc.sync.dma_start(out=bcol[:], in_=b.rearrange("(G p t) -> p G t", p=P, t=4))
+            nc.sync.dma_start(out=gcol[:], in_=g.rearrange("(G p t) -> p G t", p=P, t=4))
+            nc.sync.dma_start(out=lall[:], in_=l.rearrange("(p h) k -> p h k", h=2))
             nc.sync.dma_start(out=w2c[:].bitcast(I32), in_=w2_words.rearrange("g p n -> p g n").bitcast(I32))
             load_scales(nc.sync, w2s, w2_scales)
-            widen(0, 0, 0, S)
-            widen(0, 0, 1, V)
             widen(0, 1, 0, S)
-            widen(0, 1, 1, S)
-            turn(jrow[0][0], B[0])
+            warm_pe(B[0])
+            warm_pe(B[0])
+            warm_pe(B[1])
+            widen(0, 0, 0, S)
+            widen(0, 1, 1, V)
+            widen(0, 0, 1, V)
             permute_words(0)
+            warm_pe(B[2])
+            warm_pe(B[3])
+            warm_pe(B[4])
+            turn_j(0, 1, B[5])
             permute_scales(0)
-            widen(0, 2, 0, V)
+            warm_pe(B[6])
+            warm_pe(B[7])
+            turn(xrow[0], B[0])
+            empty(jgrp[0][:, :, 1], B[5], S)
+            widen(0, 2, 1, S)
+            empty(xgrp[:, 0], B[0], S)
+            turn(xrow[1], B[1])
+            warm_pe(B[2])
+            warm_pe(B[3])
+            empty(xgrp[:, 1], B[1], S)
             widen(0, 3, 1, V)
-            widen(0, 3, 0, S)
-            turn(xrow[0], B[1])
-            empty(xgrp[:, 0], B[1], S)
-            widen(0, 2, 1, V)
-            turn(jrow[0][1], B[2])
-            widen(1, 0, 0, V)
-            turn(xrow[1], B[3])
-            widen(1, 2, 1, V)
-            turn(jrow[0][3], B[4])
-            widen(1, 2, 0, V)
-            widen(1, 0, 1, S)
-            empty(jgrp[0][:, :, 3], B[4], S)
-            gains()
-            turn(jrow[0][2], B[5])
-            turn(jrow[1][0], B[6])
-            turn(jrow[1][2], B[7])
-            empty(xgrp[:, 1], B[3], S)
-            turn(lrow[0], B[1])
-            widen(1, 3, 1, V)
-            widen(1, 1, 1, V)
-            widen(1, 3, 0, V)
-            empty(jgrp[1][:, :, 0], B[6], S)
-            turn(lrow[1], B[4])
-            quant_x(1)
-            turn(jrow[1][3], B[3])
-            widen(1, 1, 0, V)
-            empty(jgrp[0][:, :, 2], B[5], S)
-            empty(jgrp[1][:, :, 2], B[7], S)
+            widen(0, 3, 0, V)
+            widen(0, 2, 0, V)
+            turn_j(0, 0, B[4])
             quant_x(0)
-            turn(jrow[1][1], B[6])
-            empty(jgrp[0][:, :, 0], B[0], S)
-            mm_a(0, 0, B[5])
-            empty(jgrp[0][:, :, 1], B[2], S)
-            permute_scales(1)
+            quant_x(1)
             permute_words(1)
-            empty(jgrp[1][:, :, 3], B[3], S)
-            mm_a(0, 1, B[7])
-            quant_j(0, 1)
+            turn_j(0, 2, B[6])
+            widen(1, 2, 1, V)
+            gains()
+            empty(jgrp[0][:, :, 0], B[4], S)
+            permute_scales(1)
+            turn_j(0, 3, B[7])
+            empty(jgrp[0][:, :, 2], B[6], S)
+            empty(jgrp[0][:, :, 3], B[7], S)
+            mm_a(0, 1, B[5])
+            mm_a(0, 0, B[0])
             quant_j(0, 0)
-            tanh(0, 0, B[5])
-            mm_a(1, 1, B[0])
-            mm_a(1, 0, B[2])
-            empty(jgrp[1][:, :, 1], B[6], S)
-            quant_j(1, 1)
-            mm_j(0, 0, 0, B[3])
-            tanh(0, 1, B[7])
-            square_th(0, 0)
-            quant_j(1, 0)
-            mm_jt(0, 1, 2, B[5])
-            tanh(1, 1, B[0])
-            square_j(0, 0, 0, B[3])
-            gain_th(0, 1)
-            empty(lgrp[:, 1], B[4], V)
-            tanh(1, 0, B[2])
-            slope(0, 0, V)
-            mm_j(1, 0, 2, B[6])
-            mm_j(0, 0, 3, B[7])
-            mm_j(0, 0, 1, B[0])
-            empty(lgrp[:, 0], B[1], S)
-            mm_j(0, 0, 2, B[3])
-            square_j(0, 0, 1, B[0])
-            gain_th(0, 0)
-            gain_th(1, 0)
-            quant_th(0)
-            square_th(0, 1)
-            mm_jt(0, 1, 0, B[4])
-            quant_l(0)
-            slope(0, 1, V)
-            mm_j(1, 0, 3, B[2])
-            gain_th(1, 1)
+            quant_j(0, 1)
+            turn(lrow[1], B[2])
+            widen(1, 3, 0, V)
+            widen(1, 1, 1, V)
+            turn(lrow[0], B[3])
+            tanh(0, 1, B[5])
+            widen(1, 2, 0, V)
+            widen(1, 3, 1, V)
+            tanh(0, 0, B[0])
+            mm_a(1, 0, B[1])
+            widen(1, 0, 0, V)
+            mm_j(0, 0, 3, B[4])
+            gain_th(0, 1, S)
+            mm_jt(0, 1, 2, B[6])
+            mm_a(1, 1, B[7])
+            empty(lgrp[:, 1], B[2], S)
+            mm_j(0, 0, 2, B[5])
+            turn_j(1, 2, B[0])
+            gain_th(0, 0, S)
+            tanh(1, 0, B[1])
+            empty(lgrp[:, 0], B[3], S)
+            widen(1, 0, 1, V)
+            square_j(0, 0, 3, B[4])
+            turn_j(1, 3, B[2])
+            tanh(1, 1, B[7])
+            widen(1, 1, 0, V)
             quant_l(1)
-            square_j(0, 0, 3, B[7])
-            mm_jt(1, 1, 3, B[1])
-            mm_jt(1, 1, 0, B[0])
-            square_j(1, 0, 2, B[6])
-            add_pairs(0, 0, 0)
-            mm_j(1, 0, 0, B[7])
-            square_j(0, 0, 2, B[3])
-            square_j(1, 0, 3, B[2])
-            quant_th(1)
-            square_j(1, 0, 0, B[7])
-            mm_j(1, 0, 1, B[6])
-            add_pairs(1, 0, 1)
-            mm_l(0, 0, B[3])
-            mm_jt(1, 1, 2, B[2])
-            square_j(1, 0, 1, B[6])
-            add_pairs(0, 0, 1)
-            square_jt(0, 1, 2, B[5])
-            add_pairs(1, 0, 0)
-            square_jt(0, 1, 0, B[4])
-            mm_jt(0, 1, 1, B[7])
-            square_th(1, 0)
-            add_halves(0, 0, slice(0, 4))
-            mm_jt(1, 1, 1, B[6])
+            empty(jgrp[1][:, :, 3], B[2], S)
+            gain_th(1, 0, V)
+            quant_l(0)
+            turn_j(1, 1, B[1])
+            turn_j(1, 0, B[3])
+            square_j(0, 0, 2, B[5])
+            empty(jgrp[1][:, :, 1], B[1], S)
+            empty(jgrp[1][:, :, 2], B[0], V)
+            square_jt(0, 1, 2, B[6])
+            gain_th(1, 1, V)
+            mm_l(1, 0, B[4])
+            empty(jgrp[1][:, :, 0], B[3], V)
+            quant_j(1, 1)
+            quant_j(1, 0)
+            weave_th(1)
+            square_th(0, 0)
+            mm_l(0, 0, B[7])
+            mm_j(0, 0, 0, B[2])
+            square_th(0, 1)
             mm_jt(0, 1, 3, B[5])
-            square_jt(0, 1, 1, B[7])
-            add_halves(1, 0, slice(0, 4))
-            curve(0, 0, slice(0, 4))
-            curve(1, 0, slice(0, 4))
-            mm_y(1, 0, B[4])
+            mm_j(0, 0, 1, B[1])
+            weave_th(0)
+            add_pairs(0, 0, 1)
+            quant_th(1)
+            mm_j(1, 0, 0, B[0])
+            mm_j(1, 0, 1, B[6])
+            square_j(0, 0, 0, B[2])
+            square_j(0, 0, 1, B[1])
+            mm_j(1, 0, 3, B[3])
+            add_pairs(0, 0, 0)
+            square_j(1, 0, 0, B[0])
+            mm_j(1, 0, 2, B[2])
+            mm_jt(0, 1, 0, B[1])
+            square_j(1, 0, 1, B[6])
+            square_j(1, 0, 3, B[3])
+            quant_th(0)
+            square_j(1, 0, 2, B[2])
+            mm_jt(0, 1, 1, B[0])
+            square_jt(0, 1, 0, B[1])
             square_jt(0, 1, 3, B[5])
-            mm_l(1, 0, B[7])
-            square_jt(1, 1, 3, B[1])
-            mm_l(0, 1, B[5])
-            add_la(0, 0, B[3], slice(0, 4))
-            square_jt(1, 1, 0, B[0])
-            add_la(1, 0, B[7], slice(0, 4))
-            sum_turn(0, 1, B[1], slice(0, 4))
-            square_jt(1, 1, 2, B[2])
+            add_halves(0, 0, slice(0, 4))
+            add_pairs(1, 0, 0)
+            mm_jt(1, 1, 1, B[6])
+            mm_jt(1, 1, 3, B[3])
+            square_jt(0, 1, 1, B[0])
+            slope(0, 0, S)
+            mm_jt(1, 1, 2, B[2])
+            curve(0, 0, slice(0, 4))
+            square_jt(1, 1, 3, B[3])
             square_jt(1, 1, 1, B[6])
-            sum_turn(1, 1, B[3], slice(0, 4))
-            slope(1, 0, S)
-            mm_y(1, 1, B[0])
+            add_pairs(1, 0, 1)
+            mm_jt(1, 1, 0, B[1])
+            add_la(0, 0, B[7], slice(0, 4))
+            sum_turn(0, 1, B[5], slice(0, 4))
+            add_halves(1, 0, slice(0, 4))
+            slope(0, 1, V)
+            mm_l(0, 1, B[0])
+            curve(1, 0, slice(0, 4))
+            square_jt(1, 1, 2, B[2])
+            square_jt(1, 1, 0, B[1])
             square_th(1, 1)
-            mm_l(1, 1, B[7])
-            store(out_y, 1, 0, B[4], 2, S)
             gain_lh(0, 0)
-            mm_y(0, 0, B[2])
-            gain_lh(1, 0)
             slope(1, 1, S)
-            mm_y(0, 1, B[6])
+            mm_y(0, 0, B[3])
+            add_la(1, 0, B[4], slice(0, 4))
+            sum_turn(1, 1, B[6], slice(0, 4))
+            curve_ps(0, 1, B[5], slice(0, 4))
+            square_th(1, 0)
             quant_lh(0, 0)
-            curve_ps(0, 1, B[1], slice(0, 4))
-            quant_lh(1, 0)
-            add_la(0, 1, B[5], slice(0, 4))
-            curve_ps(1, 1, B[3], slice(0, 4))
+            gain_lh(1, 0)
+            mm_l(1, 1, B[7])
+            mm_y(0, 1, B[2])
+            slope(1, 0, S)
+            add_la(0, 1, B[0], slice(0, 4))
+            mm_y(1, 0, B[1])
+            curve_ps(1, 1, B[6], slice(0, 4))
             gain_lh(0, 1)
-            mm_lap(0, 0, 0, B[1])
             add_la(1, 1, B[7], slice(0, 4))
-            store(out_y, 1, 1, B[0], 3, S)
+            mm_lap(0, 0, 0, B[4])
             quant_lh(0, 1)
-            store(out_y, 0, 0, B[2], 0, S)
-            mm_lap(0, 1, 0, B[4])
-            mm_lap(0, 0, 1, B[1])
-            mm_lap(1, 0, 0, B[5])
-            mm_lap(0, 1, 1, B[4])
+            mm_y(1, 1, B[5])
+            mm_lap(0, 1, 0, B[0])
+            quant_lh(1, 0)
+            mm_lap(0, 0, 1, B[4])
+            store(out_y, 0, 0, B[3], 0, S)
+            mm_lap(0, 1, 1, B[0])
+            store(out_y, 0, 1, B[2], 1, S)
+            mm_lap(1, 1, 0, B[6])
+            store(out_y, 1, 0, B[1], 2, S)
             gain_lh(1, 1)
-            store(out_y, 0, 1, B[6], 1, S)
-            store(out_lap, 0, 0, B[1], 4, S)
+            store(out_y, 1, 1, B[5], 3, S)
             quant_lh(1, 1)
-            mm_lap(1, 0, 1, B[5])
-            mm_lap(1, 1, 0, B[3])
-            store(out_lap, 0, 1, B[4], 5, V)
-            store(out_lap, 1, 0, B[5], 6, S)
-            mm_lap(1, 1, 1, B[3])
-            store(out_lap, 1, 1, B[3], 7, S)
+            mm_lap(1, 0, 0, B[7])
+            mm_lap(1, 1, 1, B[6])
+            store(out_lap, 0, 0, B[4], 4, S)
+            mm_lap(1, 0, 1, B[7])
+            store(out_lap, 0, 1, B[0], 5, V)
+            store(out_lap, 1, 1, B[6], 7, S)
+            store(out_lap, 1, 0, B[7], 6, V)

from contextlib import ExitStack

import concourse.mybir as mybir
from concourse.masks import make_identity

F32 = mybir.dt.float32
BF16 = mybir.dt.bfloat16
U8 = mybir.dt.uint8
I32 = mybir.dt.int32
U32 = mybir.dt.uint32
FP8 = mybir.dt.float8_e4m3fn
FP8X4 = mybir.dt.float8_e4m3fn_x4
FP4X4 = mybir.dt.float4_e2m1fn_x4
ALU = mybir.AluOpType
ACT = mybir.ActivationFunctionType

P = 128
TOKENS, COORDS, D, F, OUT = 256, 4, 1024, 1024, 1024
FLOPS = 2 * (COORDS + 2) * TOKENS * D * F + 2 * 2 * TOKENS * F * OUT


def tile_forwardlaplaciantanhlayer_d1p_kernel(
    tc, x, j_bytes, j_scale, l, w1_words, w1_scales, b, g, w2_words, w2_scales, out_lap, out_y
):
    nc = tc.nc
    with ExitStack() as ctx:
        sb = ctx.enter_context(tc.tile_pool(name="sb", bufs=1))
        ps = ctx.enter_context(tc.psum_pool(name="ps", bufs=1))

        def tile(name, shape, dtype):
            return sb.tile(shape, dtype, name=name, align_bytes=64)

        banks = [ps.tile([P, 512], F32, name="bank%d" % i) for i in range(8)]

        ident = tile("ident", [P, P], F32)
        warm = tile("warm", [P, 2], F32)
        jsc = tile("jsc", [P, COORDS, 2, 8], F32)
        jraw = [[tile("jraw%d%d" % (h, cp), [P, 2, D], U8) for cp in range(2)] for h in range(2)]
        jrow = [[tile("jrow%d%d" % (h, c), [P, D], BF16) for c in range(COORDS)] for h in range(2)]
        xall = tile("xall", [P, 2, D], BF16)
        xrow = [xall[:, h] for h in range(2)]
        lall = tile("lall", [P, 2, D], BF16)
        lrow = [lall[:, h] for h in range(2)]
        xgrp = tile("xgrp", [P, 2, 2, P, 4], BF16)
        lgrp = tile("lgrp", [P, 2, 2, P, 4], BF16)
        jgrp = [tile("jgrp%d" % h, [P, 2, COORDS, P, 4], BF16) for h in range(2)]
        xc, xs = tile("xc", [P, 2, 2, P], U32), tile("xs", [P, 2, 2, P], U8)
        lc, ls = tile("lc", [P, 2, 2, P], U32), tile("ls", [P, 2, 2, P], U8)
        jc = [tile("jc%d" % h, [P, 2, COORDS * P], U32) for h in range(2)]
        js = [tile("js%d" % h, [P, 2, COORDS * P], U8) for h in range(2)]
        w1raw = [tile("w1raw%d" % G, [P, 2, 1024], U8) for G in range(2)]
        w1sraw = tile("w1sraw", [P, 2, F], U8)
        w1c = [tile("w1c%d" % G, [P, 2, 4, 2 * P], U8) for G in range(2)]
        w1s = [tile("w1s%d" % G, [P, 2, 4, P], U8) for G in range(2)]
        w2c = tile("w2c", [P, 2, 2 * OUT], U8)
        w2s = tile("w2s", [P, 2, OUT], U8)
        bcol = tile("bcol", [P, 2, 4], BF16)
        gcol = tile("gcol", [P, 2, 4], BF16)
        gpos = tile("gpos", [P, 2, 4], F32)
        gneg = tile("gneg", [P, 2, 4], F32)
        th = [tile("th%d" % G, [P, 4, TOKENS], F32) for G in range(2)]
        th2 = [tile("th2%d" % G, [P, 4, TOKENS], F32) for G in range(2)]
        d1g = [tile("d1g%d" % G, [P, 4, TOKENS], F32) for G in range(2)]
        thp = tile("thp", [P, 2, 4, TOKENS], BF16)
        zeros = tile("zeros", [P, 512], BF16)
        thg = tile("thg", [P, 2, TOKENS, 4], BF16)
        tc_, ts_ = tile("thc", [P, 2, TOKENS], U32), tile("ths", [P, 2, TOKENS], U8)
        sqr = [[tile("sqr%d%d" % (h, G), [P, 4, COORDS, P], F32) for G in range(2)] for h in range(2)]
        half = [[tile("half%d%d" % (h, G), [P, 4, 2, P], F32) for G in range(2)] for h in range(2)]
        ssum = [[tile("ssum%d%d" % (h, G), [P, 4, P], F32) for G in range(2)] for h in range(2)]
        prod = [[tile("prod%d%d" % (h, G), [P, 4, P], F32) for G in range(2)] for h in range(2)]
        inner = [[tile("inner%d%d" % (h, G), [P, 4, P], F32) for G in range(2)] for h in range(2)]
        lhg = [tile("lhg%d" % h, [P, 2, P, 4], BF16) for h in range(2)]
        hc = [tile("hc%d" % h, [P, 2, P], U32) for h in range(2)]
        hs = [tile("hs%d" % h, [P, 2, P], U8) for h in range(2)]
        res = [tile("res%d" % i, [P, 512], F32) for i in range(8)]

        def rows(h):
            return slice(h * P, (h + 1) * P)

        def load_scales(eng, plane, scales):
            for q in range(4):
                eng.dma_start(
                    out=plane[32 * q : 32 * q + 4, :, :].bitcast(I32),
                    in_=scales[:, 4 * q : 4 * q + 4, :].rearrange("g r n -> r g n").bitcast(I32),
                )

        def load_j(h, cp):
            nc.sync.dma_start(out=jraw[h][cp][:], in_=j_bytes[2 * cp : 2 * cp + 2].rearrange("c (p h) k -> p c h k", h=2)[:, :, h, :])

        def load_w1(G):
            nc.sync.dma_start(
                out=w1raw[G][:].bitcast(I32),
                in_=w1_words[:, :, 1024 * G : 1024 * (G + 1)].rearrange("g p n -> p g n").bitcast(I32),
            )

        def permute_words(G):
            nc.vector.tensor_copy(
                out=w1c[G][:].rearrange("p g t (m e) -> p g t m e", e=2),
                in_=w1raw[G][:].rearrange("p g (m t e) -> p g t m e", t=4, e=2),
            )

        def permute_scales(G):
            nc.vector.tensor_copy(
                out=w1s[G][:], in_=w1sraw[:, :, 512 * G : 512 * (G + 1)].rearrange("p g (m t) -> p g t m", t=4)
            )

        split = set()

        def turn_j(h, c, bank):
            words = jrow[h][c][:].bitcast(F32)
            for gp in range(2):
                for u in range(2):
                    s = 2 * gp + u
                    src = words[:, s * P : (s + 1) * P] if (h, c, gp) in split else words[:, 256 * gp + u : 256 * (gp + 1) : 2]
                    nc.tensor.transpose(bank[:, s * P : (s + 1) * P], src, ident[:])

        def widen(h, c, gp, on_vector):
            for i in range(4 * gp, 4 * gp + 4):
                cols = slice(i * P, (i + 1) * P)
                src = jraw[h][c // 2][:, c % 2, cols].bitcast(FP8)
                scale = jsc[:, c, h, i : i + 1]
                if on_vector:
                    split.add((h, c, gp))
                    dst = jrow[h][c][:, 512 * gp : 512 * (gp + 1)].rearrange("p (u m e) -> p m u e", u=2, e=2)
                    nc.vector.tensor_scalar(
                        out=dst[:, 32 * (i % 4) : 32 * (i % 4 + 1)], in0=src.rearrange("p (m u e) -> p m u e", u=2, e=2),
                        scalar1=scale, scalar2=None, op0=ALU.mult,
                    )
                else:
                    nc.scalar.activation(out=jrow[h][c][:, cols], in_=src, func=ACT.Copy, scale=scale)

        def turn(row, bank):
            words = row[:].bitcast(F32)
            for gp in range(2):
                for u in range(2):
                    s = 2 * gp + u
                    nc.tensor.transpose(bank[:, s * P : (s + 1) * P], words[:, 256 * gp + u : 256 * (gp + 1) : 2], ident[:])

        def empty(dst, bank, on_vector):
            out = dst.bitcast(F32)
            src = bank[:].rearrange("p (g u r) -> p g r u", g=2, u=2)
            if on_vector:
                nc.vector.tensor_copy(out=out, in_=src)
            else:
                nc.scalar.copy(out=out, in_=src)

        def quant(codes, scales, src):
            nc.vector.quantize_mx(out=codes.bitcast(FP8X4), scales=scales, in_=src)

        def stage1(out, G, t, codes, scales):
            for gp in range(2):
                nc.tensor.matmul_mx(
                    out=out,
                    lhsT=w1c[G][:, gp, t, :].bitcast(FP4X4),
                    lhsT_scale=w1s[G][:, gp, t, :],
                    rhs=codes[:, gp, :].bitcast(FP8X4),
                    rhs_scale=scales[:, gp, :],
                    start=(gp == 0),
                    stop=(gp == 1),
                )

        def mm_a(G, tp, bank):
            for t in (2 * tp, 2 * tp + 1):
                for h in range(2):
                    s = 2 * (t % 2) + h
                    stage1(bank[:, s * P : (s + 1) * P], G, t, xc[:, h], xs[:, h])

        def tanh(G, tp, bank):
            for t in (2 * tp, 2 * tp + 1):
                nc.scalar.activation(
                    out=th[G][:, t, :], in_=bank[:, (t % 2) * 256 : (t % 2 + 1) * 256], func=ACT.Tanh, bias=bcol[:, G, t : t + 1]
                )

        def square_th(G, tp):
            ts = slice(2 * tp, 2 * tp + 2)
            nc.scalar.activation(out=th2[G][:, ts], in_=th[G][:, ts], func=ACT.Square)

        def slope(G, tp, on_vector):
            for t in (2 * tp, 2 * tp + 1):
                neg, pos = gneg[:, G, t : t + 1], gpos[:, G, t : t + 1]
                if on_vector:
                    nc.vector.tensor_scalar(
                        out=d1g[G][:, t, :], in0=th2[G][:, t, :], scalar1=neg, scalar2=pos, op0=ALU.mult, op1=ALU.add
                    )
                else:
                    nc.scalar.activation(out=d1g[G][:, t, :], in_=th2[G][:, t, :], func=ACT.Identity, scale=neg, bias=pos)

        def gains():
            nc.vector.tensor_copy(out=gpos[:], in_=gcol[:])
            nc.vector.tensor_scalar(out=gneg[:], in0=gcol[:], scalar1=-1.0, scalar2=None, op0=ALU.mult)

        def gain_th(G, tp, on_vector):
            for t in (2 * tp, 2 * tp + 1):
                pos = gpos[:, G, t : t + 1]
                if on_vector:
                    nc.vector.tensor_scalar(out=thp[:, G, t, :], in0=th[G][:, t, :], scalar1=pos, scalar2=None, op0=ALU.mult)
                else:
                    nc.scalar.activation(out=thp[:, G, t, :], in_=th[G][:, t, :], func=ACT.Copy, scale=pos)

        def weave_th(G):
            nc.vector.tensor_copy(
                out=thg[:, G].rearrange("p (c i) t -> p c t i", i=4), in_=thp[:, G].rearrange("p t (c i) -> p c t i", i=4)
            )

        def warm_pe(bank):
            nc.tensor.matmul(bank[:], lhsT=zeros[:, 0:P], rhs=zeros[:], start=True, stop=True)

        def quant_th(G):
            quant(tc_[:, G, :], ts_[:, G, :], thg[:, G].rearrange("p r t -> p (r t)"))

        def quant_x(h):
            quant(xc[:, h].rearrange("p g r -> p (g r)"), xs[:, h].rearrange("p g r -> p (g r)"), flat(xgrp[:, h]))

        def mm_l(h, G, bank):
            for t in range(4):
                stage1(bank[:, t * P : (t + 1) * P], G, t, lc[:, h], ls[:, h])

        def mm_j(h, G, t, bank):
            stage1(bank[:], G, t, jc[h], js[h])

        def square_j(h, G, t, bank):
            nc.scalar.activation(out=sqr[h][G][:, t].rearrange("p c r -> p (c r)"), in_=bank[:], func=ACT.Square)

        def mm_jt(h, G, c, bank):
            for gp in range(2):
                nc.tensor.matmul_mx(
                    out=bank[:],
                    lhsT=jc[h][:, gp, c * P : (c + 1) * P].bitcast(FP8X4),
                    lhsT_scale=js[h][:, gp, c * P : (c + 1) * P],
                    rhs=w1raw[G][:, gp, :].bitcast(FP4X4),
                    rhs_scale=w1sraw[:, gp, 512 * G : 512 * (G + 1)],
                    start=(gp == 0),
                    stop=(gp == 1),
                )

        def square_jt(h, G, c, bank):
            nc.scalar.activation(out=sqr[h][G][:, c], in_=bank[:].rearrange("p (m t) -> p t m", t=4), func=ACT.Square)

        def sum_turn(h, G, bank, ts):
            for t in range(ts.start, ts.stop):
                for c in range(COORDS):
                    nc.tensor.matmul(
                        bank[:, t * P : (t + 1) * P], lhsT=sqr[h][G][:, c, t, :], rhs=ident[:], start=(c == 0), stop=(c == COORDS - 1),
                        is_transpose=True,
                    )

        def curve_ps(h, G, bank, ts):
            nc.vector.scalar_tensor_tensor(
                out=prod[h][G][:, ts], in0=bank[:].rearrange("p (t r) -> p t r", t=4)[:, ts], scalar=-2.0, in1=th[G][:, ts, rows(h)],
                op0=ALU.mult, op1=ALU.mult,
            )

        def add_pairs(h, G, tp):
            ts = slice(2 * tp, 2 * tp + 2)
            nc.vector.tensor_tensor(out=half[h][G][:, ts], in0=sqr[h][G][:, ts, 0:2], in1=sqr[h][G][:, ts, 2:4], op=ALU.add)

        def add_halves(h, G, ts):
            nc.vector.tensor_tensor(out=ssum[h][G][:, ts], in0=half[h][G][:, ts, 0], in1=half[h][G][:, ts, 1], op=ALU.add)

        def curve(h, G, ts):
            nc.vector.scalar_tensor_tensor(
                out=prod[h][G][:, ts], in0=ssum[h][G][:, ts], scalar=-2.0, in1=th[G][:, ts, rows(h)], op0=ALU.mult, op1=ALU.mult
            )

        def add_la(h, G, bank, ts):
            nc.vector.tensor_tensor(
                out=inner[h][G][:, ts], in0=bank[:].rearrange("p (t r) -> p t r", t=4)[:, ts], in1=prod[h][G][:, ts], op=ALU.add
            )

        def gain_lh(h, G):
            nc.vector.tensor_tensor(
                out=lhg[h][:, G].rearrange("p (c i) t -> p c t i", i=4),
                in0=inner[h][G][:].rearrange("p t (c i) -> p c t i", i=4),
                in1=d1g[G][:, :, rows(h)].rearrange("p t (c i) -> p c t i", i=4),
                op=ALU.mult,
            )

        def stage2(bank, codes, scales, nh, G):
            nc.tensor.matmul_mx(
                out=bank[:],
                lhsT=codes.bitcast(FP8X4),
                lhsT_scale=scales,
                rhs=w2c[:, G, 1024 * nh : 1024 * (nh + 1)].bitcast(FP4X4),
                rhs_scale=w2s[:, G, 512 * nh : 512 * (nh + 1)],
                start=(G == 0),
                stop=(G == 1),
            )

        def mm_y(h, nh, bank):
            for G in range(2):
                stage2(bank, tc_[:, G, rows(h)], ts_[:, G, rows(h)], nh, G)

        def mm_lap(h, nh, G, bank):
            stage2(bank, hc[h][:, G, :], hs[h][:, G, :], nh, G)

        def store(dst, h, nh, bank, slot, on_vector):
            if on_vector:
                nc.vector.tensor_copy(out=res[slot][:], in_=bank[:])
            else:
                nc.scalar.copy(out=res[slot][:], in_=bank[:])
            nc.sync.dma_start(out=dst.rearrange("(p h) n -> p h n", h=2)[:, h, 512 * nh : 512 * (nh + 1)], in_=res[slot][:])

        def flat(ap):
            return ap.rearrange("p a r t -> p (a r t)")

        def quant_j(h, gp):
            quant(jc[h][:, gp, :], js[h][:, gp, :], flat(jgrp[h][:, gp]))

        def quant_l(h):
            quant(lc[:, h].rearrange("p g r -> p (g r)"), ls[:, h].rearrange("p g r -> p (g r)"), flat(lgrp[:, h]))

        def quant_lh(h, G):
            quant(hc[h][:, G, :], hs[h][:, G, :], lhg[h][:, G].rearrange("p r t -> p (r t)"))

        B = banks
        V, S = True, False
        with tc.manual_schedule():
            nc.vector.memset(zeros[:], 0.0)
            nc.vector.memset(w1sraw[:].bitcast(U32), 0)
            nc.vector.memset(ident[:], 0.0)
            nc.vector.memset(w2s[:].bitcast(U32), 0)
            nc.sync.dma_start(out=jsc[:], in_=j_scale.rearrange("c (p h) i -> p c h i", h=2))
            load_j(0, 0)
            load_w1(0)
            nc.sync.dma_start(out=xall[:], in_=x.rearrange("(p h) k -> p h k", h=2))
            load_scales(nc.scalar, w1sraw, w1_scales)
            nc.scalar.activation(out=warm[:, 0:1], in_=zeros[:, 0:1], func=ACT.Tanh)
            make_identity(nc, ident[:], nomemset=True)
            load_j(0, 1)
            load_w1(1)
            load_j(1, 0)
            load_j(1, 1)
            nc.sync.dma_start(out=bcol[:], in_=b.rearrange("(G p t) -> p G t", p=P, t=4))
            nc.sync.dma_start(out=gcol[:], in_=g.rearrange("(G p t) -> p G t", p=P, t=4))
            nc.sync.dma_start(out=lall[:], in_=l.rearrange("(p h) k -> p h k", h=2))
            nc.sync.dma_start(out=w2c[:].bitcast(I32), in_=w2_words.rearrange("g p n -> p g n").bitcast(I32))
            load_scales(nc.sync, w2s, w2_scales)
            widen(0, 1, 0, S)
            warm_pe(B[0])
            warm_pe(B[0])
            warm_pe(B[1])
            widen(0, 0, 0, S)
            widen(0, 1, 1, V)
            widen(0, 0, 1, V)
            permute_words(0)
            warm_pe(B[2])
            warm_pe(B[3])
            warm_pe(B[4])
            turn_j(0, 1, B[5])
            permute_scales(0)
            warm_pe(B[6])
            warm_pe(B[7])
            turn(xrow[0], B[0])
            empty(jgrp[0][:, :, 1], B[5], S)
            widen(0, 2, 1, S)
            empty(xgrp[:, 0], B[0], S)
            turn(xrow[1], B[1])
            warm_pe(B[2])
            warm_pe(B[3])
            empty(xgrp[:, 1], B[1], S)
            widen(0, 3, 1, V)
            widen(0, 3, 0, V)
            widen(0, 2, 0, V)
            turn_j(0, 0, B[4])
            quant_x(0)
            quant_x(1)
            permute_words(1)
            turn_j(0, 2, B[6])
            widen(1, 2, 1, V)
            gains()
            empty(jgrp[0][:, :, 0], B[4], S)
            permute_scales(1)
            turn_j(0, 3, B[7])
            empty(jgrp[0][:, :, 2], B[6], S)
            empty(jgrp[0][:, :, 3], B[7], S)
            mm_a(0, 1, B[5])
            mm_a(0, 0, B[0])
            quant_j(0, 0)
            quant_j(0, 1)
            turn(lrow[1], B[2])
            widen(1, 3, 0, V)
            widen(1, 1, 1, V)
            turn(lrow[0], B[3])
            tanh(0, 1, B[5])
            widen(1, 2, 0, V)
            widen(1, 3, 1, V)
            tanh(0, 0, B[0])
            mm_a(1, 0, B[1])
            widen(1, 0, 0, V)
            mm_j(0, 0, 3, B[4])
            gain_th(0, 1, S)
            mm_jt(0, 1, 2, B[6])
            mm_a(1, 1, B[7])
            empty(lgrp[:, 1], B[2], S)
            mm_j(0, 0, 2, B[5])
            turn_j(1, 2, B[0])
            gain_th(0, 0, S)
            tanh(1, 0, B[1])
            empty(lgrp[:, 0], B[3], S)
            widen(1, 0, 1, V)
            square_j(0, 0, 3, B[4])
            turn_j(1, 3, B[2])
            tanh(1, 1, B[7])
            widen(1, 1, 0, V)
            quant_l(1)
            empty(jgrp[1][:, :, 3], B[2], S)
            gain_th(1, 0, V)
            quant_l(0)
            turn_j(1, 1, B[1])
            turn_j(1, 0, B[3])
            square_j(0, 0, 2, B[5])
            empty(jgrp[1][:, :, 1], B[1], S)
            empty(jgrp[1][:, :, 2], B[0], V)
            square_jt(0, 1, 2, B[6])
            gain_th(1, 1, V)
            mm_l(1, 0, B[4])
            empty(jgrp[1][:, :, 0], B[3], V)
            quant_j(1, 1)
            quant_j(1, 0)
            weave_th(1)
            square_th(0, 0)
            mm_l(0, 0, B[7])
            mm_j(0, 0, 0, B[2])
            square_th(0, 1)
            mm_jt(0, 1, 3, B[5])
            mm_j(0, 0, 1, B[1])
            weave_th(0)
            add_pairs(0, 0, 1)
            quant_th(1)
            mm_j(1, 0, 0, B[0])
            mm_j(1, 0, 1, B[6])
            square_j(0, 0, 0, B[2])
            square_j(0, 0, 1, B[1])
            mm_j(1, 0, 3, B[3])
            add_pairs(0, 0, 0)
            square_j(1, 0, 0, B[0])
            mm_j(1, 0, 2, B[2])
            mm_jt(0, 1, 0, B[1])
            square_j(1, 0, 1, B[6])
            square_j(1, 0, 3, B[3])
            quant_th(0)
            square_j(1, 0, 2, B[2])
            mm_jt(0, 1, 1, B[0])
            square_jt(0, 1, 0, B[1])
            square_jt(0, 1, 3, B[5])
            add_halves(0, 0, slice(0, 4))
            add_pairs(1, 0, 0)
            mm_jt(1, 1, 1, B[6])
            mm_jt(1, 1, 3, B[3])
            square_jt(0, 1, 1, B[0])
            slope(0, 0, S)
            mm_jt(1, 1, 2, B[2])
            curve(0, 0, slice(0, 4))
            square_jt(1, 1, 3, B[3])
            square_jt(1, 1, 1, B[6])
            add_pairs(1, 0, 1)
            mm_jt(1, 1, 0, B[1])
            add_la(0, 0, B[7], slice(0, 4))
            sum_turn(0, 1, B[5], slice(0, 4))
            add_halves(1, 0, slice(0, 4))
            slope(0, 1, V)
            mm_l(0, 1, B[0])
            curve(1, 0, slice(0, 4))
            square_jt(1, 1, 2, B[2])
            square_jt(1, 1, 0, B[1])
            square_th(1, 1)
            gain_lh(0, 0)
            slope(1, 1, S)
            mm_y(0, 0, B[3])
            add_la(1, 0, B[4], slice(0, 4))
            sum_turn(1, 1, B[6], slice(0, 4))
            curve_ps(0, 1, B[5], slice(0, 4))
            square_th(1, 0)
            quant_lh(0, 0)
            gain_lh(1, 0)
            mm_l(1, 1, B[7])
            mm_y(0, 1, B[2])
            slope(1, 0, S)
            add_la(0, 1, B[0], slice(0, 4))
            mm_y(1, 0, B[1])
            curve_ps(1, 1, B[6], slice(0, 4))
            gain_lh(0, 1)
            add_la(1, 1, B[7], slice(0, 4))
            mm_lap(0, 0, 0, B[4])
            quant_lh(0, 1)
            mm_y(1, 1, B[5])
            mm_lap(0, 1, 0, B[0])
            quant_lh(1, 0)
            mm_lap(0, 0, 1, B[4])
            store(out_y, 0, 0, B[3], 0, S)
            mm_lap(0, 1, 1, B[0])
            store(out_y, 0, 1, B[2], 1, S)
            mm_lap(1, 1, 0, B[6])
            store(out_y, 1, 0, B[1], 2, S)
            gain_lh(1, 1)
            store(out_y, 1, 1, B[5], 3, S)
            quant_lh(1, 1)
            mm_lap(1, 0, 0, B[7])
            mm_lap(1, 1, 1, B[6])
            store(out_lap, 0, 0, B[4], 4, S)
            mm_lap(1, 0, 1, B[7])
            store(out_lap, 0, 1, B[0], 5, V)
            store(out_lap, 1, 1, B[6], 7, S)
            store(out_lap, 1, 0, B[7], 6, V)
